import numpy as np
CORES = [4,132,260,388,12,140,268,396,20,148,276,404,28,156,284,412]
N = 16
PERM = [[0,4],[1,5],[2,6],[3,7],[4,8],[5,9],[6,10],[7,11],[8,12],[9,13],[10,14],[11,15],[12,0],[13,1],[14,2],[15,3]]
def setup_inputs(rng):
    return {"x": rng.standard_normal((N, 128, 256), dtype=np.float32)}
def reference(x):
    y = np.empty_like(x)
    for s, d in PERM:
        y[d] = x[s]
    return {"y": y}

@@ -1,0 +1,46 @@
+from concourse.bass import DstId, RemoteDMATransfer
+
+HELPERS = (6, 2, 7, 3)
+P = 4
+
+SCRATCH = {
+    "stage": ("dram", [P, 128, 64], "float32"),
+    "land": ("dram", [P, 128, 64], "float32"),
+}
+SEMAPHORES = ["loaded", "sent", "arrived", "stored"]
+
+
+def rank_program(g, core, T, topo):
+    home = (core // 8) * 8 + 4
+    src_rank = T.rank_of(home)
+    if src_rank is None:
+        return
+    dst_of = dict((s, d) for s, d in T.tables["PERM"])
+    target = T.cores[dst_of[src_rank]]
+    local = core % 8
+
+    if local in HELPERS:
+        t = HELPERS.index(local)
+        rid, pid = topo.addr(target, core)
+        g.wait_ge(T.sem.arrived, 4)
+        g.remote_dma(T.land[t], T.land[t], T.sem.arrived, T.sem.sent, pid, rid, 0x00FF)
+        g.wait_ge(T.sem.sent, 8)
+        return
+
+    if core != home:
+        return
+
+    g.sync.dma_start(T.stage[:], T.x[:]).then_inc(T.sem.loaded, 16)
+    g.wait_ge(T.sem.loaded, 16)
+    transfers = []
+    for t in range(P):
+        h = home - 4 + HELPERS[t]
+        rid, pid = topo.addr(h, core)
+        transfers.append(RemoteDMATransfer(dst_ids=[DstId(rid=rid, pnc=pid)], dma_engine_mask=0xF << (4 * t),
+                                           remote_sem=T.sem.arrived, src=T.stage[t], dst=T.land[t]))
+    g.remote_dma_fused(transfers, local_sem=T.sem.sent)
+
+    g.sync.wait_ge(T.sem.arrived, 8 * P)
+    g.sync.dma_start(T.y[:], T.land[:]).then_inc(T.sem.stored, 16)
+    g.wait_ge(T.sem.sent, 16)
+    g.wait_ge(T.sem.stored, 16)

@@ -7,7 +7,7 @@ SCRATCH = {
     "stage": ("dram", [P, 128, 64], "float32"),
     "land": ("dram", [P, 128, 64], "float32"),
 }
-SEMAPHORES = ["loaded", "sent", "arrived", "stored"]
+SEMAPHORES = ["load0", "load1", "sent", "arr0", "arr1", "stored"]
 
 
 def rank_program(g, core, T, topo):
@@ -22,25 +22,28 @@ def rank_program(g, core, T, topo):
     if local in HELPERS:
         t = HELPERS.index(local)
         rid, pid = topo.addr(target, core)
-        g.wait_ge(T.sem.arrived, 4)
-        g.remote_dma(T.land[t], T.land[t], T.sem.arrived, T.sem.sent, pid, rid, 0x00FF)
+        g.wait_ge(T.sem.arr0, 8)
+        g.remote_dma(T.land[t], T.land[t], T.sem["arr%d" % (t // 2)], T.sem.sent, pid, rid, 0x00FF)
         g.wait_ge(T.sem.sent, 8)
         return
 
     if core != home:
         return
 
-    g.sync.dma_start(T.stage[:], T.x[:]).then_inc(T.sem.loaded, 16)
-    g.wait_ge(T.sem.loaded, 16)
-    transfers = []
-    for t in range(P):
-        h = home - 4 + HELPERS[t]
-        rid, pid = topo.addr(h, core)
-        transfers.append(RemoteDMATransfer(dst_ids=[DstId(rid=rid, pnc=pid)], dma_engine_mask=0xF << (4 * t),
-                                           remote_sem=T.sem.arrived, src=T.stage[t], dst=T.land[t]))
-    g.remote_dma_fused(transfers, local_sem=T.sem.sent)
-
-    g.sync.wait_ge(T.sem.arrived, 8 * P)
-    g.sync.dma_start(T.y[:], T.land[:]).then_inc(T.sem.stored, 16)
-    g.wait_ge(T.sem.sent, 16)
-    g.wait_ge(T.sem.stored, 16)
+    queues = (g.sync, g.scalar)
+    for w in range(2):
+        queues[w].dma_start(T.stage[2 * w:2 * w + 2], T.x[64 * w:64 * w + 64, :]).then_inc(T.sem["load%d" % w], 16)
+    for w in range(2):
+        transfers = []
+        for k in range(2):
+            t = 2 * w + k
+            rid, pid = topo.addr(home - 4 + HELPERS[t], core)
+            transfers.append(RemoteDMATransfer(dst_ids=[DstId(rid=rid, pnc=pid)], dma_engine_mask=0xFF << (8 * k),
+                                               remote_sem=T.sem.arr0, src=T.stage[t], dst=T.land[t]))
+        g.wait_ge(T.sem["load%d" % w], 16)
+        g.remote_dma_fused(transfers, local_sem=T.sem.sent)
+    for w in range(2):
+        queues[w].wait_ge(T.sem["arr%d" % w], 16)
+        queues[w].dma_start(T.y[64 * w:64 * w + 64, :], T.land[2 * w:2 * w + 2]).then_inc(T.sem.stored, 16)
+    g.wait_ge(T.sem.sent, 32)
+    g.wait_ge(T.sem.stored, 32)

@@ -1,13 +1,13 @@
-from concourse.bass import DstId, RemoteDMATransfer
-
+ROWS = (48, 36, 28, 16)
 HELPERS = (6, 2, 7, 3)
-P = 4
+W = 4
+START = tuple(sum(ROWS[:w]) for w in range(W + 1))
 
-SCRATCH = {
-    "stage": ("dram", [P, 128, 64], "float32"),
-    "land": ("dram", [P, 128, 64], "float32"),
-}
-SEMAPHORES = ["load0", "load1", "sent", "arr0", "arr1", "stored"]
+SCRATCH = {}
+for _w in range(W):
+    SCRATCH["stage%d" % _w] = ("dram", [128, 2 * ROWS[_w]], "float32")
+    SCRATCH["land%d" % _w] = ("dram", [128, 2 * ROWS[_w]], "float32")
+SEMAPHORES = (["load%d" % w for w in range(W)] + ["arr%d" % w for w in range(W)] + ["sent", "stored"])
 
 
 def rank_program(g, core, T, topo):
@@ -20,10 +20,11 @@ def rank_program(g, core, T, topo):
     local = core % 8
 
     if local in HELPERS:
-        t = HELPERS.index(local)
+        w = HELPERS.index(local)
         rid, pid = topo.addr(target, core)
-        g.wait_ge(T.sem.arr0, 8)
-        g.remote_dma(T.land[t], T.land[t], T.sem["arr%d" % (t // 2)], T.sem.sent, pid, rid, 0x00FF)
+        land = T["land%d" % w]
+        g.wait_ge(T.sem["arr%d" % w], 16)
+        g.remote_dma(land[:], land[:], T.sem["arr%d" % w], T.sem.sent, pid, rid, 0x00FF)
         g.wait_ge(T.sem.sent, 8)
         return
 
@@ -31,19 +32,14 @@ def rank_program(g, core, T, topo):
         return
 
     queues = (g.sync, g.scalar)
-    for w in range(2):
-        queues[w].dma_start(T.stage[2 * w:2 * w + 2], T.x[64 * w:64 * w + 64, :]).then_inc(T.sem["load%d" % w], 16)
-    for w in range(2):
-        transfers = []
-        for k in range(2):
-            t = 2 * w + k
-            rid, pid = topo.addr(home - 4 + HELPERS[t], core)
-            transfers.append(RemoteDMATransfer(dst_ids=[DstId(rid=rid, pnc=pid)], dma_engine_mask=0xFF << (8 * k),
-                                               remote_sem=T.sem.arr0, src=T.stage[t], dst=T.land[t]))
+    for w in range(W):
+        queues[w % 2].dma_start(T["stage%d" % w][:], T.x[START[w]:START[w + 1], :]).then_inc(T.sem["load%d" % w], 16)
+    for w in range(W):
+        rid, pid = topo.addr(home - 4 + HELPERS[w], core)
         g.wait_ge(T.sem["load%d" % w], 16)
-        g.remote_dma_fused(transfers, local_sem=T.sem.sent)
-    for w in range(2):
-        queues[w].wait_ge(T.sem["arr%d" % w], 16)
-        queues[w].dma_start(T.y[64 * w:64 * w + 64, :], T.land[2 * w:2 * w + 2]).then_inc(T.sem.stored, 16)
-    g.wait_ge(T.sem.sent, 32)
-    g.wait_ge(T.sem.stored, 32)
+        g.remote_dma(T["land%d" % w][:], T["stage%d" % w][:], T.sem["arr%d" % w], T.sem.sent, pid, rid, 0xFFFF)
+    for w in range(W):
+        queues[w % 2].wait_ge(T.sem["arr%d" % w], 8)
+        queues[w % 2].dma_start(T.y[START[w]:START[w + 1], :], T["land%d" % w][:]).then_inc(T.sem.stored, 16)
+    g.wait_ge(T.sem.sent, 16 * W)
+    g.wait_ge(T.sem.stored, 16 * W)

ROWS = (48, 36, 28, 16)
HELPERS = (6, 2, 7, 3)
W = 4
START = tuple(sum(ROWS[:w]) for w in range(W + 1))

SCRATCH = {}
for _w in range(W):
    SCRATCH["stage%d" % _w] = ("dram", [128, 2 * ROWS[_w]], "float32")
    SCRATCH["land%d" % _w] = ("dram", [128, 2 * ROWS[_w]], "float32")
SEMAPHORES = (["load%d" % w for w in range(W)] + ["arr%d" % w for w in range(W)] + ["sent", "stored"])


def rank_program(g, core, T, topo):
    home = (core // 8) * 8 + 4
    src_rank = T.rank_of(home)
    if src_rank is None:
        return
    dst_of = dict((s, d) for s, d in T.tables["PERM"])
    target = T.cores[dst_of[src_rank]]
    local = core % 8

    if local in HELPERS:
        w = HELPERS.index(local)
        rid, pid = topo.addr(target, core)
        land = T["land%d" % w]
        g.wait_ge(T.sem["arr%d" % w], 16)
        g.remote_dma(land[:], land[:], T.sem["arr%d" % w], T.sem.sent, pid, rid, 0x00FF)
        g.wait_ge(T.sem.sent, 8)
        return

    if core != home:
        return

    queues = (g.sync, g.scalar)
    for w in range(W):
        queues[w % 2].dma_start(T["stage%d" % w][:], T.x[START[w]:START[w + 1], :]).then_inc(T.sem["load%d" % w], 16)
    for w in range(W):
        rid, pid = topo.addr(home - 4 + HELPERS[w], core)
        g.wait_ge(T.sem["load%d" % w], 16)
        g.remote_dma(T["land%d" % w][:], T["stage%d" % w][:], T.sem["arr%d" % w], T.sem.sent, pid, rid, 0xFFFF)
    for w in range(W):
        queues[w % 2].wait_ge(T.sem["arr%d" % w], 8)
        queues[w % 2].dma_start(T.y[START[w]:START[w + 1], :], T["land%d" % w][:]).then_inc(T.sem.stored, 16)
    g.wait_ge(T.sem.sent, 16 * W)
    g.wait_ge(T.sem.stored, 16 * W)
